import numpy as np
import ml_dtypes


def mxq(x, axis, fmt="e4m3"):
    dtype, down = {"e4m3": (ml_dtypes.float8_e4m3fn, 7), "e5m2": (ml_dtypes.float8_e5m2, 14)}[fmt]
    v = np.moveaxis(np.asarray(x, np.float32).astype(ml_dtypes.bfloat16).astype(np.float64), axis, -1)
    blocks = v.reshape(v.shape[:-1] + (-1, 32))
    amax = np.abs(blocks).max(-1, keepdims=True)
    byte = np.maximum(np.where(amax > 0, np.frexp(amax)[1] - 1 + 127, 0) - down, 1)
    scale = np.exp2(byte - 127.0)
    codes = (blocks / scale).astype(np.float32).astype(dtype).astype(np.float64)
    return np.moveaxis((codes * scale).reshape(v.shape), -1, axis)


WIDE = False


def mx_kscale(k):
    if not WIDE:
        return np.ones(k)
    levels = np.array([10, -10, 5, -5, 0])
    if k % 512:
        return np.exp2(np.random.permutation(np.resize(levels, k // 32))).repeat(32)
    a = np.empty((k // 512, 16))
    for p in range(k // 512):
        a[p, :8] = np.random.permutation(np.resize(levels, 8))
        for g in range(8):
            far = levels[np.abs(levels - a[p, g]) >= 10]
            a[p, g + 8] = far[np.random.randint(len(far))]
    return np.exp2(a.ravel()).repeat(32)


def f64(x):
    return np.asarray(x).astype(np.float64)


def striped(idx):
    return np.tile(idx.reshape(-1, 16).T, (8, 1)).astype(np.uint16)


def unstriped(offs):
    return offs[:16].T.reshape(-1).astype(np.int64)


def gelu(v):
    return 0.5 * v * (1.0 + np.tanh(np.sqrt(2.0 / np.pi) * (v + 0.044715 * v**3)))


K, T, S, N, U = 512, 2048, 1024, 128, 2048


def setup_inputs():
    n = np.random.standard_normal
    s = mx_kscale(K)[:, None]
    return {
        "xT": (n((K, T)) * s).astype(np.float32),
        "w1": (n((K, N)) / np.sqrt(K) / s).astype(np.float32),
        "res": n((N, U)).astype(np.float32),
        "offs": striped(np.random.permutation(T)[:S]),
        "own": striped(np.random.randint(0, S, U)),
    }


def reference(xT, w1, res, offs, own):
    xq = mxq(f64(xT)[:, unstriped(offs)], 0, "e4m3")
    y = gelu(mxq(f64(w1), 0, "e4m3").T @ xq)
    return f64(res) + y[:, unstriped(own)]

@@ -1,0 +1,123 @@
+from contextlib import ExitStack
+
+import concourse.mybir as mybir
+
+K, T, S, N, U = 512, 2048, 1024, 128, 2048
+FLOPS = 2 * K * N * S
+
+F32 = mybir.dt.float32
+BF16 = mybir.dt.bfloat16
+U32 = mybir.dt.uint32
+U16 = mybir.dt.uint16
+U8 = mybir.dt.uint8
+FP8X4 = mybir.dt.float8_e4m3fn_x4
+ACT = mybir.ActivationFunctionType
+
+P = 128
+PACK = 4
+LIST = 16
+VECTOR_PICKS = 384
+CHUNKS = [(1024, 1024), (1024, 1024), (1024, 1024), (1024, 768, 256)]
+SCALAR_LAST = (384, 256)
+GROUPS = ((256, 128), (256, 128), (256,))
+OUT_PIECES = (512, 512, 512, 384, 128)
+
+
+def tile_picked_unmerge_gelu_e_kernel(tc, xT, w1, res, offs, own, out):
+    nc = tc.nc
+    with ExitStack() as ctx:
+        keep = ctx.enter_context(tc.tile_pool(name="keep", bufs=1))
+        psum = ctx.enter_context(tc.psum_pool(name="psum", bufs=1))
+
+        offs_t = keep.tile([P, S // LIST], U16, name="offs_t")
+        own_t = keep.tile([P, U // LIST], U16, name="own_t")
+        nc.sync.dma_start(offs_t[:], offs)
+
+        warm = keep.tile([P, 8], F32, name="warm")
+        warm_out = keep.tile([P, 8], F32, name="warm_out")
+        nc.vector.memset(warm[:], 0.0)
+        nc.scalar.activation(warm_out[:], warm[:], ACT.Gelu_apprx_tanh)
+
+        x_rows = xT.rearrange("(p j) t -> p j t", j=PACK)
+        x_f32 = [keep.tile([P, T], F32, name="x_f32_%d" % j) for j in range(PACK)]
+        x_bf16 = [keep.tile([P, T], BF16, name="x_bf16_%d" % j) for j in range(PACK)]
+        for j in range(PACK):
+            c0 = 0
+            for width in CHUNKS[j]:
+                nc.sync.dma_start(x_f32[j][:, c0 : c0 + width], x_rows[:, j, c0 : c0 + width])
+                c0 = c0 + width
+        w_f32 = keep.tile([P, PACK, N], F32, name="w_f32")
+        nc.sync.dma_start(w_f32[:], w1.rearrange("(p j) n -> p j n", j=PACK))
+        nc.sync.dma_start(own_t[:], own)
+        res_t = keep.tile([P, U], F32, name="res_t")
+        for h in range(2):
+            nc.sync.dma_start(res_t[:, h * 1024 : (h + 1) * 1024], res[:, h * 1024 : (h + 1) * 1024])
+
+        picked_v = keep.tile([P, VECTOR_PICKS * PACK], BF16, name="picked_v", align_bytes=64)
+        picked_s = keep.tile([P, (S - VECTOR_PICKS) * PACK], BF16, name="picked_s", align_bytes=64)
+        slots_v = picked_v[:].rearrange("p (n j) -> p n j", j=PACK)
+        slots_s = picked_s[:].rearrange("p (n j) -> p n j", j=PACK)
+
+        for j in range(PACK):
+            c0 = 0
+            for width in CHUNKS[j]:
+                nc.vector.tensor_copy(x_bf16[j][:, c0 : c0 + width], x_f32[j][:, c0 : c0 + width])
+                c0 = c0 + width
+            nc.vector.tensor_copy(slots_v[:, :, j], x_f32[j][:].indirect(offs_t[:, 0 : VECTOR_PICKS // LIST]))
+            n0 = 0
+            for count in SCALAR_LAST if j == PACK - 1 else (S - VECTOR_PICKS,):
+                e0 = VECTOR_PICKS + n0
+                nc.scalar.activation(
+                    slots_s[:, n0 : n0 + count, j],
+                    x_bf16[j][:].indirect(offs_t[:, e0 // LIST : (e0 + count) // LIST]),
+                    ACT.Copy,
+                )
+                n0 = n0 + count
+
+        w_bf16 = keep.tile([P, N, PACK], BF16, name="w_bf16", align_bytes=64)
+        w_codes = keep.tile([P, N], U32, name="w_codes", align_bytes=64)
+        w_scales = keep.tile([P, N], U8, name="w_scales", align_bytes=64)
+        nc.vector.tensor_copy(w_bf16[:], w_f32[:].rearrange("p j n -> p n j"))
+        nc.vector.quantize_mx(
+            out=w_codes[:].bitcast(FP8X4), scales=w_scales[:], in_=w_bf16[:].rearrange("p n j -> p (n j)")
+        )
+
+        y = keep.tile([P, S], F32, name="y")
+        e0 = 0
+        for g, widths in enumerate(GROUPS):
+            total = sum(widths)
+            acc = psum.tile([P, total], F32, name="acc_%d" % g)
+            c0 = 0
+            for i, width in enumerate(widths):
+                codes = keep.tile([P, width], U32, name="codes_%d_%d" % (g, i), align_bytes=64)
+                scales = keep.tile([P, width], U8, name="scales_%d_%d" % (g, i), align_bytes=64)
+                e = e0 + c0
+                if e < VECTOR_PICKS:
+                    source = picked_v[:, e * PACK : (e + width) * PACK]
+                else:
+                    source = picked_s[:, (e - VECTOR_PICKS) * PACK : (e - VECTOR_PICKS + width) * PACK]
+                nc.vector.quantize_mx(out=codes[:].bitcast(FP8X4), scales=scales[:], in_=source)
+                nc.tensor.matmul_mx(
+                    out=acc[:, c0 : c0 + width],
+                    lhsT=w_codes[:].bitcast(FP8X4),
+                    lhsT_scale=w_scales[:],
+                    rhs=codes[:].bitcast(FP8X4),
+                    rhs_scale=scales[:],
+                    start=True,
+                    stop=True,
+                )
+                c0 = c0 + width
+            nc.scalar.activation(y[:, e0 : e0 + total], acc[:], ACT.Gelu_apprx_tanh)
+            e0 = e0 + total
+
+        r0 = 0
+        for i, width in enumerate(OUT_PIECES):
+            summed = keep.tile([P, width], F32, name="summed_%d" % i)
+            nc.vector.tensor_tensor(
+                summed[:],
+                y[:].indirect(own_t[:, r0 // LIST : (r0 + width) // LIST]),
+                res_t[:, r0 : r0 + width],
+                mybir.AluOpType.add,
+            )
+            nc.sync.dma_start(out[:, r0 : r0 + width], summed[:])
+            r0 = r0 + width

@@ -16,11 +16,11 @@ ACT = mybir.ActivationFunctionType
 P = 128
 PACK = 4
 LIST = 16
-VECTOR_PICKS = 384
+VECTOR_PICKS = (352, 352, 384, 384)
 CHUNKS = [(1024, 1024), (1024, 1024), (1024, 1024), (1024, 768, 256)]
-SCALAR_LAST = (384, 256)
-GROUPS = ((256, 128), (256, 128), (256,))
-OUT_PIECES = (512, 512, 512, 384, 128)
+SCALAR_LAST = (768, 1024)
+GROUPS = ((256,), (256,), (256,), (128, 128))
+OUT_PIECES = (512, 512, 512, 256, 128, 128)
 
 
 def tile_picked_unmerge_gelu_e_kernel(tc, xT, w1, res, offs, own, out):
@@ -31,7 +31,6 @@ def tile_picked_unmerge_gelu_e_kernel(tc, xT, w1, res, offs, own, out):
 
         offs_t = keep.tile([P, S // LIST], U16, name="offs_t")
         own_t = keep.tile([P, U // LIST], U16, name="own_t")
-        nc.sync.dma_start(offs_t[:], offs)
 
         warm = keep.tile([P, 8], F32, name="warm")
         warm_out = keep.tile([P, 8], F32, name="warm_out")
@@ -45,42 +44,42 @@ def tile_picked_unmerge_gelu_e_kernel(tc, xT, w1, res, offs, own, out):
             c0 = 0
             for width in CHUNKS[j]:
                 nc.sync.dma_start(x_f32[j][:, c0 : c0 + width], x_rows[:, j, c0 : c0 + width])
+                if j == 0 and c0 == 0:
+                    nc.sync.dma_start(offs_t[:], offs)
                 c0 = c0 + width
-        w_f32 = keep.tile([P, PACK, N], F32, name="w_f32")
+        w_f32 = keep.tile([P, PACK, N], F32, name="w_f32", tag="w_then_codes", align_bytes=64)
         nc.sync.dma_start(w_f32[:], w1.rearrange("(p j) n -> p j n", j=PACK))
         nc.sync.dma_start(own_t[:], own)
         res_t = keep.tile([P, U], F32, name="res_t")
         for h in range(2):
             nc.sync.dma_start(res_t[:, h * 1024 : (h + 1) * 1024], res[:, h * 1024 : (h + 1) * 1024])
 
-        picked_v = keep.tile([P, VECTOR_PICKS * PACK], BF16, name="picked_v", align_bytes=64)
-        picked_s = keep.tile([P, (S - VECTOR_PICKS) * PACK], BF16, name="picked_s", align_bytes=64)
-        slots_v = picked_v[:].rearrange("p (n j) -> p n j", j=PACK)
-        slots_s = picked_s[:].rearrange("p (n j) -> p n j", j=PACK)
+        picked = keep.tile([P, S * PACK], BF16, name="picked", align_bytes=64)
+        slots = picked[:].rearrange("p (n j) -> p n j", j=PACK)
 
         for j in range(PACK):
             c0 = 0
             for width in CHUNKS[j]:
-                nc.vector.tensor_copy(x_bf16[j][:, c0 : c0 + width], x_f32[j][:, c0 : c0 + width])
+                if j == PACK - 1 and c0 + width == T:
+                    nc.scalar.copy(x_bf16[j][:, c0 : c0 + width], x_f32[j][:, c0 : c0 + width])
+                else:
+                    nc.vector.tensor_copy(x_bf16[j][:, c0 : c0 + width], x_f32[j][:, c0 : c0 + width])
                 c0 = c0 + width
-            nc.vector.tensor_copy(slots_v[:, :, j], x_f32[j][:].indirect(offs_t[:, 0 : VECTOR_PICKS // LIST]))
-            n0 = 0
-            for count in SCALAR_LAST if j == PACK - 1 else (S - VECTOR_PICKS,):
-                e0 = VECTOR_PICKS + n0
+            share = VECTOR_PICKS[j]
+            nc.vector.tensor_copy(slots[:, 0:share, j], x_f32[j][:].indirect(offs_t[:, 0 : share // LIST]))
+            e0 = share
+            for e1 in SCALAR_LAST if j == PACK - 1 else (S,):
                 nc.scalar.activation(
-                    slots_s[:, n0 : n0 + count, j],
-                    x_bf16[j][:].indirect(offs_t[:, e0 // LIST : (e0 + count) // LIST]),
+                    slots[:, e0:e1, j],
+                    x_bf16[j][:].indirect(offs_t[:, e0 // LIST : e1 // LIST]),
                     ACT.Copy,
                 )
-                n0 = n0 + count
+                e0 = e1
 
         w_bf16 = keep.tile([P, N, PACK], BF16, name="w_bf16", align_bytes=64)
         w_codes = keep.tile([P, N], U32, name="w_codes", align_bytes=64)
         w_scales = keep.tile([P, N], U8, name="w_scales", align_bytes=64)
         nc.vector.tensor_copy(w_bf16[:], w_f32[:].rearrange("p j n -> p n j"))
-        nc.vector.quantize_mx(
-            out=w_codes[:].bitcast(FP8X4), scales=w_scales[:], in_=w_bf16[:].rearrange("p n j -> p (n j)")
-        )
 
         y = keep.tile([P, S], F32, name="y")
         e0 = 0
@@ -89,14 +88,24 @@ def tile_picked_unmerge_gelu_e_kernel(tc, xT, w1, res, offs, own, out):
             acc = psum.tile([P, total], F32, name="acc_%d" % g)
             c0 = 0
             for i, width in enumerate(widths):
-                codes = keep.tile([P, width], U32, name="codes_%d_%d" % (g, i), align_bytes=64)
+                codes = keep.tile(
+                    [P, width],
+                    U32,
+                    name="codes_%d_%d" % (g, i),
+                    tag="w_then_codes" if g + i == 0 else "codes_%d_%d" % (g, i),
+                    align_bytes=64,
+                )
                 scales = keep.tile([P, width], U8, name="scales_%d_%d" % (g, i), align_bytes=64)
                 e = e0 + c0
-                if e < VECTOR_PICKS:
-                    source = picked_v[:, e * PACK : (e + width) * PACK]
-                else:
-                    source = picked_s[:, (e - VECTOR_PICKS) * PACK : (e - VECTOR_PICKS + width) * PACK]
-                nc.vector.quantize_mx(out=codes[:].bitcast(FP8X4), scales=scales[:], in_=source)
+                nc.vector.quantize_mx(
+                    out=codes[:].bitcast(FP8X4), scales=scales[:], in_=picked[:, e * PACK : (e + width) * PACK]
+                )
+                if g + i == 0:
+                    nc.vector.quantize_mx(
+                        out=w_codes[:].bitcast(FP8X4),
+                        scales=w_scales[:],
+                        in_=w_bf16[:].rearrange("p n j -> p (n j)"),
+                    )
                 nc.tensor.matmul_mx(
                     out=acc[:, c0 : c0 + width],
                     lhsT=w_codes[:].bitcast(FP8X4),

@@ -16,10 +16,12 @@ ACT = mybir.ActivationFunctionType
 P = 128
 PACK = 4
 LIST = 16
-VECTOR_PICKS = (352, 352, 384, 384)
-CHUNKS = [(1024, 1024), (1024, 1024), (1024, 1024), (1024, 768, 256)]
+VECTOR_PICKS = (320, 352, 320, 352)
+CHUNKS = [(2048,), (1536, 512), (1536, 512), (1024, 768, 256)]
 SCALAR_LAST = (768, 1024)
-GROUPS = ((256,), (256,), (256,), (128, 128))
+GROUPS = ((256,), (256,), (256,), (128,), (128,))
+SLOT = (0, 2, 1, 3)
+FIRST_CAST_SPLIT = 1376
 OUT_PIECES = (512, 512, 512, 256, 128, 128)
 
 
@@ -43,7 +45,7 @@ def tile_picked_unmerge_gelu_e_kernel(tc, xT, w1, res, offs, own, out):
         for j in range(PACK):
             c0 = 0
             for width in CHUNKS[j]:
-                nc.sync.dma_start(x_f32[j][:, c0 : c0 + width], x_rows[:, j, c0 : c0 + width])
+                nc.sync.dma_start(x_f32[j][:, c0 : c0 + width], x_rows[:, SLOT[j], c0 : c0 + width])
                 if j == 0 and c0 == 0:
                     nc.sync.dma_start(offs_t[:], offs)
                 c0 = c0 + width
@@ -59,24 +61,25 @@ def tile_picked_unmerge_gelu_e_kernel(tc, xT, w1, res, offs, own, out):
 
         for j in range(PACK):
             c0 = 0
-            for width in CHUNKS[j]:
-                if j == PACK - 1 and c0 + width == T:
-                    nc.scalar.copy(x_bf16[j][:, c0 : c0 + width], x_f32[j][:, c0 : c0 + width])
-                else:
+            if j == 0:
+                nc.vector.tensor_copy(x_bf16[j][:, :FIRST_CAST_SPLIT], x_f32[j][:, :FIRST_CAST_SPLIT])
+                nc.scalar.copy(x_bf16[j][:, FIRST_CAST_SPLIT:], x_f32[j][:, FIRST_CAST_SPLIT:])
+            else:
+                for width in CHUNKS[j]:
                     nc.vector.tensor_copy(x_bf16[j][:, c0 : c0 + width], x_f32[j][:, c0 : c0 + width])
-                c0 = c0 + width
+                    c0 = c0 + width
             share = VECTOR_PICKS[j]
-            nc.vector.tensor_copy(slots[:, 0:share, j], x_f32[j][:].indirect(offs_t[:, 0 : share // LIST]))
+            nc.vector.tensor_copy(slots[:, 0:share, SLOT[j]], x_f32[j][:].indirect(offs_t[:, 0 : share // LIST]))
             e0 = share
             for e1 in SCALAR_LAST if j == PACK - 1 else (S,):
                 nc.scalar.activation(
-                    slots[:, e0:e1, j],
+                    slots[:, e0:e1, SLOT[j]],
                     x_bf16[j][:].indirect(offs_t[:, e0 // LIST : e1 // LIST]),
                     ACT.Copy,
                 )
                 e0 = e1
 
-        w_bf16 = keep.tile([P, N, PACK], BF16, name="w_bf16", align_bytes=64)
+        w_bf16 = keep.tile([P, N, PACK], BF16, name="w_bf16", tag="w_bf16_then_codes", align_bytes=64)
         w_codes = keep.tile([P, N], U32, name="w_codes", align_bytes=64)
         w_scales = keep.tile([P, N], U8, name="w_scales", align_bytes=64)
         nc.vector.tensor_copy(w_bf16[:], w_f32[:].rearrange("p j n -> p n j"))
@@ -88,17 +91,17 @@ def tile_picked_unmerge_gelu_e_kernel(tc, xT, w1, res, offs, own, out):
             acc = psum.tile([P, total], F32, name="acc_%d" % g)
             c0 = 0
             for i, width in enumerate(widths):
-                codes = keep.tile(
-                    [P, width],
-                    U32,
-                    name="codes_%d_%d" % (g, i),
-                    tag="w_then_codes" if g + i == 0 else "codes_%d_%d" % (g, i),
-                    align_bytes=64,
-                )
+                if g + i == 0:
+                    first_codes = keep.tile([P, width], U32, name="first_codes", tag="w_then_codes", align_bytes=64)
+                    codes = first_codes[:]
+                else:
+                    if g + i == 1:
+                        later_codes = keep.tile([P, S], U32, name="later_codes", tag="w_bf16_then_codes", align_bytes=64)
+                    codes = later_codes[:, e0 + c0 : e0 + c0 + width]
                 scales = keep.tile([P, width], U8, name="scales_%d_%d" % (g, i), align_bytes=64)
                 e = e0 + c0
                 nc.vector.quantize_mx(
-                    out=codes[:].bitcast(FP8X4), scales=scales[:], in_=picked[:, e * PACK : (e + width) * PACK]
+                    out=codes.bitcast(FP8X4), scales=scales[:], in_=picked[:, e * PACK : (e + width) * PACK]
                 )
                 if g + i == 0:
                     nc.vector.quantize_mx(
@@ -110,7 +113,7 @@ def tile_picked_unmerge_gelu_e_kernel(tc, xT, w1, res, offs, own, out):
                     out=acc[:, c0 : c0 + width],
                     lhsT=w_codes[:].bitcast(FP8X4),
                     lhsT_scale=w_scales[:],
-                    rhs=codes[:].bitcast(FP8X4),
+                    rhs=codes.bitcast(FP8X4),
                     rhs_scale=scales[:],
                     start=True,
                     stop=True,

@@ -16,12 +16,11 @@ ACT = mybir.ActivationFunctionType
 P = 128
 PACK = 4
 LIST = 16
-VECTOR_PICKS = (320, 352, 320, 352)
-CHUNKS = [(2048,), (1536, 512), (1536, 512), (1024, 768, 256)]
+VECTOR_PICKS = (320, 288, 320, 288)
+CHUNKS = [(1280, 768), (1280, 768), (1280, 768), (1024, 768, 256)]
 SCALAR_LAST = (768, 1024)
 GROUPS = ((256,), (256,), (256,), (128,), (128,))
 SLOT = (0, 2, 1, 3)
-FIRST_CAST_SPLIT = 1376
 OUT_PIECES = (512, 512, 512, 256, 128, 128)
 
 
@@ -34,10 +33,10 @@ def tile_picked_unmerge_gelu_e_kernel(tc, xT, w1, res, offs, own, out):
         offs_t = keep.tile([P, S // LIST], U16, name="offs_t")
         own_t = keep.tile([P, U // LIST], U16, name="own_t")
 
-        warm = keep.tile([P, 8], F32, name="warm")
-        warm_out = keep.tile([P, 8], F32, name="warm_out")
-        nc.vector.memset(warm[:], 0.0)
-        nc.scalar.activation(warm_out[:], warm[:], ACT.Gelu_apprx_tanh)
+        zero = keep.tile([P, 1], F32, name="zero")
+        zero_bias = keep.tile([P, 1], F32, name="zero_bias")
+        nc.vector.memset(zero[:], 0.0)
+        nc.scalar.activation(zero_bias[:], zero[:], ACT.Gelu_apprx_tanh)
 
         x_rows = xT.rearrange("(p j) t -> p j t", j=PACK)
         x_f32 = [keep.tile([P, T], F32, name="x_f32_%d" % j) for j in range(PACK)]
@@ -46,7 +45,7 @@ def tile_picked_unmerge_gelu_e_kernel(tc, xT, w1, res, offs, own, out):
             c0 = 0
             for width in CHUNKS[j]:
                 nc.sync.dma_start(x_f32[j][:, c0 : c0 + width], x_rows[:, SLOT[j], c0 : c0 + width])
-                if j == 0 and c0 == 0:
+                if j == 0 and c0 > 0:
                     nc.sync.dma_start(offs_t[:], offs)
                 c0 = c0 + width
         w_f32 = keep.tile([P, PACK, N], F32, name="w_f32", tag="w_then_codes", align_bytes=64)
@@ -61,13 +60,9 @@ def tile_picked_unmerge_gelu_e_kernel(tc, xT, w1, res, offs, own, out):
 
         for j in range(PACK):
             c0 = 0
-            if j == 0:
-                nc.vector.tensor_copy(x_bf16[j][:, :FIRST_CAST_SPLIT], x_f32[j][:, :FIRST_CAST_SPLIT])
-                nc.scalar.copy(x_bf16[j][:, FIRST_CAST_SPLIT:], x_f32[j][:, FIRST_CAST_SPLIT:])
-            else:
-                for width in CHUNKS[j]:
-                    nc.vector.tensor_copy(x_bf16[j][:, c0 : c0 + width], x_f32[j][:, c0 : c0 + width])
-                    c0 = c0 + width
+            for width in CHUNKS[j]:
+                nc.vector.tensor_copy(x_bf16[j][:, c0 : c0 + width], x_f32[j][:, c0 : c0 + width])
+                c0 = c0 + width
             share = VECTOR_PICKS[j]
             nc.vector.tensor_copy(slots[:, 0:share, SLOT[j]], x_f32[j][:].indirect(offs_t[:, 0 : share // LIST]))
             e0 = share
@@ -119,7 +114,7 @@ def tile_picked_unmerge_gelu_e_kernel(tc, xT, w1, res, offs, own, out):
                     stop=True,
                 )
                 c0 = c0 + width
-            nc.scalar.activation(y[:, e0 : e0 + total], acc[:], ACT.Gelu_apprx_tanh)
+            nc.scalar.activation(y[:, e0 : e0 + total], acc[:], ACT.Gelu_apprx_tanh, bias=zero_bias[:])
             e0 = e0 + total
 
         r0 = 0

@@ -16,11 +16,11 @@ ACT = mybir.ActivationFunctionType
 P = 128
 PACK = 4
 LIST = 16
-VECTOR_PICKS = (320, 288, 320, 288)
-CHUNKS = [(1280, 768), (1280, 768), (1280, 768), (1024, 768, 256)]
+VECTOR_PICKS = (352, 352, 320, 352)
+CHUNKS = [(1280, 768), (1280, 768), (1408, 640), (1280, 512, 256)]
 SCALAR_LAST = (768, 1024)
-GROUPS = ((256,), (256,), (256,), (128,), (128,))
-SLOT = (0, 2, 1, 3)
+GROUPS = ((128,),) * 8
+SLOT = (2, 0, 1, 3)
 OUT_PIECES = (512, 512, 512, 256, 128, 128)
 
 

@@ -16,7 +16,7 @@ ACT = mybir.ActivationFunctionType
 P = 128
 PACK = 4
 LIST = 16
-VECTOR_PICKS = (352, 352, 320, 352)
+VECTOR_PICKS = (352, 320, 320, 384)
 CHUNKS = [(1280, 768), (1280, 768), (1408, 640), (1280, 512, 256)]
 SCALAR_LAST = (768, 1024)
 GROUPS = ((128,),) * 8
@@ -40,7 +40,6 @@ def tile_picked_unmerge_gelu_e_kernel(tc, xT, w1, res, offs, own, out):
 
         x_rows = xT.rearrange("(p j) t -> p j t", j=PACK)
         x_f32 = [keep.tile([P, T], F32, name="x_f32_%d" % j) for j in range(PACK)]
-        x_bf16 = [keep.tile([P, T], BF16, name="x_bf16_%d" % j) for j in range(PACK)]
         for j in range(PACK):
             c0 = 0
             for width in CHUNKS[j]:
@@ -48,7 +47,7 @@ def tile_picked_unmerge_gelu_e_kernel(tc, xT, w1, res, offs, own, out):
                 if j == 0 and c0 > 0:
                     nc.sync.dma_start(offs_t[:], offs)
                 c0 = c0 + width
-        w_f32 = keep.tile([P, PACK, N], F32, name="w_f32", tag="w_then_codes", align_bytes=64)
+        w_f32 = keep.tile([P, PACK, N], F32, name="w_f32", align_bytes=64)
         nc.sync.dma_start(w_f32[:], w1.rearrange("(p j) n -> p j n", j=PACK))
         nc.sync.dma_start(own_t[:], own)
         res_t = keep.tile([P, U], F32, name="res_t")
@@ -59,9 +58,10 @@ def tile_picked_unmerge_gelu_e_kernel(tc, xT, w1, res, offs, own, out):
         slots = picked[:].rearrange("p (n j) -> p n j", j=PACK)
 
         for j in range(PACK):
+            x_bf16 = keep.tile([P, T], BF16, name="x_bf16_%d" % j, tag="x_bf16_%d" % (j % 3))
             c0 = 0
             for width in CHUNKS[j]:
-                nc.vector.tensor_copy(x_bf16[j][:, c0 : c0 + width], x_f32[j][:, c0 : c0 + width])
+                nc.vector.tensor_copy(x_bf16[:, c0 : c0 + width], x_f32[j][:, c0 : c0 + width])
                 c0 = c0 + width
             share = VECTOR_PICKS[j]
             nc.vector.tensor_copy(slots[:, 0:share, SLOT[j]], x_f32[j][:].indirect(offs_t[:, 0 : share // LIST]))
@@ -69,7 +69,7 @@ def tile_picked_unmerge_gelu_e_kernel(tc, xT, w1, res, offs, own, out):
             for e1 in SCALAR_LAST if j == PACK - 1 else (S,):
                 nc.scalar.activation(
                     slots[:, e0:e1, SLOT[j]],
-                    x_bf16[j][:].indirect(offs_t[:, e0 // LIST : e1 // LIST]),
+                    x_bf16[:].indirect(offs_t[:, e0 // LIST : e1 // LIST]),
                     ACT.Copy,
                 )
                 e0 = e1
@@ -77,7 +77,15 @@ def tile_picked_unmerge_gelu_e_kernel(tc, xT, w1, res, offs, own, out):
         w_bf16 = keep.tile([P, N, PACK], BF16, name="w_bf16", tag="w_bf16_then_codes", align_bytes=64)
         w_codes = keep.tile([P, N], U32, name="w_codes", align_bytes=64)
         w_scales = keep.tile([P, N], U8, name="w_scales", align_bytes=64)
-        nc.vector.tensor_copy(w_bf16[:], w_f32[:].rearrange("p j n -> p n j"))
+        nc.gpsimd.tensor_scalar(
+            w_bf16[:], w_f32[:].rearrange("p j n -> p n j"), 1.0, 0.0, mybir.AluOpType.mult, mybir.AluOpType.add
+        )
+        nc.vector.quantize_mx(
+            out=w_codes[:].bitcast(FP8X4),
+            scales=w_scales[:],
+            in_=w_bf16[:].rearrange("p n j -> p (n j)"),
+        )
+        all_codes = keep.tile([P, S], U32, name="all_codes", tag="w_bf16_then_codes", align_bytes=64)
 
         y = keep.tile([P, S], F32, name="y")
         e0 = 0
@@ -86,24 +94,12 @@ def tile_picked_unmerge_gelu_e_kernel(tc, xT, w1, res, offs, own, out):
             acc = psum.tile([P, total], F32, name="acc_%d" % g)
             c0 = 0
             for i, width in enumerate(widths):
-                if g + i == 0:
-                    first_codes = keep.tile([P, width], U32, name="first_codes", tag="w_then_codes", align_bytes=64)
-                    codes = first_codes[:]
-                else:
-                    if g + i == 1:
-                        later_codes = keep.tile([P, S], U32, name="later_codes", tag="w_bf16_then_codes", align_bytes=64)
-                    codes = later_codes[:, e0 + c0 : e0 + c0 + width]
+                codes = all_codes[:, e0 + c0 : e0 + c0 + width]
                 scales = keep.tile([P, width], U8, name="scales_%d_%d" % (g, i), align_bytes=64)
                 e = e0 + c0
                 nc.vector.quantize_mx(
                     out=codes.bitcast(FP8X4), scales=scales[:], in_=picked[:, e * PACK : (e + width) * PACK]
                 )
-                if g + i == 0:
-                    nc.vector.quantize_mx(
-                        out=w_codes[:].bitcast(FP8X4),
-                        scales=w_scales[:],
-                        in_=w_bf16[:].rearrange("p n j -> p (n j)"),
-                    )
                 nc.tensor.matmul_mx(
                     out=acc[:, c0 : c0 + width],
                     lhsT=w_codes[:].bitcast(FP8X4),

@@ -12,14 +12,16 @@ U16 = mybir.dt.uint16
 U8 = mybir.dt.uint8
 FP8X4 = mybir.dt.float8_e4m3fn_x4
 ACT = mybir.ActivationFunctionType
+ALU = mybir.AluOpType
 
 P = 128
 PACK = 4
 LIST = 16
-VECTOR_PICKS = (352, 320, 320, 384)
-CHUNKS = [(1280, 768), (1280, 768), (1408, 640), (1280, 512, 256)]
-SCALAR_LAST = (768, 1024)
-GROUPS = ((128,),) * 8
+VECTOR_PICKS = (352, 352, 352, 384)
+PARTS = ((1280,768,),(1280,768,),(1408,640,),(576,704,512,256,),)
+GPSIMD_PART = (False, False, False, True)
+SCALAR_LAST = (768, 1024,)
+PIECE = 128
 SLOT = (2, 0, 1, 3)
 OUT_PIECES = (512, 512, 512, 256, 128, 128)
 
@@ -42,11 +44,11 @@ def tile_picked_unmerge_gelu_e_kernel(tc, xT, w1, res, offs, own, out):
         x_f32 = [keep.tile([P, T], F32, name="x_f32_%d" % j) for j in range(PACK)]
         for j in range(PACK):
             c0 = 0
-            for width in CHUNKS[j]:
+            for width in PARTS[j]:
                 nc.sync.dma_start(x_f32[j][:, c0 : c0 + width], x_rows[:, SLOT[j], c0 : c0 + width])
-                if j == 0 and c0 > 0:
-                    nc.sync.dma_start(offs_t[:], offs)
                 c0 = c0 + width
+            if j == 0:
+                nc.sync.dma_start(offs_t[:], offs)
         w_f32 = keep.tile([P, PACK, N], F32, name="w_f32", align_bytes=64)
         nc.sync.dma_start(w_f32[:], w1.rearrange("(p j) n -> p j n", j=PACK))
         nc.sync.dma_start(own_t[:], own)
@@ -60,8 +62,11 @@ def tile_picked_unmerge_gelu_e_kernel(tc, xT, w1, res, offs, own, out):
         for j in range(PACK):
             x_bf16 = keep.tile([P, T], BF16, name="x_bf16_%d" % j, tag="x_bf16_%d" % (j % 3))
             c0 = 0
-            for width in CHUNKS[j]:
-                nc.vector.tensor_copy(x_bf16[:, c0 : c0 + width], x_f32[j][:, c0 : c0 + width])
+            for i, width in enumerate(PARTS[j]):
+                if i == 0 and GPSIMD_PART[j]:
+                    nc.gpsimd.tensor_scalar(x_bf16[:, 0:width], x_f32[j][:, 0:width], 1.0, 0.0, ALU.mult, ALU.add)
+                else:
+                    nc.vector.tensor_copy(x_bf16[:, c0 : c0 + width], x_f32[j][:, c0 : c0 + width])
                 c0 = c0 + width
             share = VECTOR_PICKS[j]
             nc.vector.tensor_copy(slots[:, 0:share, SLOT[j]], x_f32[j][:].indirect(offs_t[:, 0 : share // LIST]))
@@ -77,9 +82,7 @@ def tile_picked_unmerge_gelu_e_kernel(tc, xT, w1, res, offs, own, out):
         w_bf16 = keep.tile([P, N, PACK], BF16, name="w_bf16", tag="w_bf16_then_codes", align_bytes=64)
         w_codes = keep.tile([P, N], U32, name="w_codes", align_bytes=64)
         w_scales = keep.tile([P, N], U8, name="w_scales", align_bytes=64)
-        nc.gpsimd.tensor_scalar(
-            w_bf16[:], w_f32[:].rearrange("p j n -> p n j"), 1.0, 0.0, mybir.AluOpType.mult, mybir.AluOpType.add
-        )
+        nc.gpsimd.tensor_scalar(w_bf16[:], w_f32[:].rearrange("p j n -> p n j"), 1.0, 0.0, ALU.mult, ALU.add)
         nc.vector.quantize_mx(
             out=w_codes[:].bitcast(FP8X4),
             scales=w_scales[:],
@@ -88,30 +91,24 @@ def tile_picked_unmerge_gelu_e_kernel(tc, xT, w1, res, offs, own, out):
         all_codes = keep.tile([P, S], U32, name="all_codes", tag="w_bf16_then_codes", align_bytes=64)
 
         y = keep.tile([P, S], F32, name="y")
-        e0 = 0
-        for g, widths in enumerate(GROUPS):
-            total = sum(widths)
-            acc = psum.tile([P, total], F32, name="acc_%d" % g)
-            c0 = 0
-            for i, width in enumerate(widths):
-                codes = all_codes[:, e0 + c0 : e0 + c0 + width]
-                scales = keep.tile([P, width], U8, name="scales_%d_%d" % (g, i), align_bytes=64)
-                e = e0 + c0
-                nc.vector.quantize_mx(
-                    out=codes.bitcast(FP8X4), scales=scales[:], in_=picked[:, e * PACK : (e + width) * PACK]
-                )
-                nc.tensor.matmul_mx(
-                    out=acc[:, c0 : c0 + width],
-                    lhsT=w_codes[:].bitcast(FP8X4),
-                    lhsT_scale=w_scales[:],
-                    rhs=codes.bitcast(FP8X4),
-                    rhs_scale=scales[:],
-                    start=True,
-                    stop=True,
-                )
-                c0 = c0 + width
-            nc.scalar.activation(y[:, e0 : e0 + total], acc[:], ACT.Gelu_apprx_tanh, bias=zero_bias[:])
-            e0 = e0 + total
+        for g in range(S // PIECE):
+            e = g * PIECE
+            acc = psum.tile([P, PIECE], F32, name="acc_%d" % g)
+            codes = all_codes[:, e : e + PIECE]
+            scales = keep.tile([P, PIECE], U8, name="scales_%d" % g, align_bytes=64)
+            nc.vector.quantize_mx(
+                out=codes.bitcast(FP8X4), scales=scales[:], in_=picked[:, e * PACK : (e + PIECE) * PACK]
+            )
+            nc.tensor.matmul_mx(
+                out=acc[:],
+                lhsT=w_codes[:].bitcast(FP8X4),
+                lhsT_scale=w_scales[:],
+                rhs=codes.bitcast(FP8X4),
+                rhs_scale=scales[:],
+                start=True,
+                stop=True,
+            )
+            nc.scalar.activation(y[:, e : e + PIECE], acc[:], ACT.Gelu_apprx_tanh, bias=zero_bias[:])
 
         r0 = 0
         for i, width in enumerate(OUT_PIECES):
@@ -120,7 +117,7 @@ def tile_picked_unmerge_gelu_e_kernel(tc, xT, w1, res, offs, own, out):
                 summed[:],
                 y[:].indirect(own_t[:, r0 // LIST : (r0 + width) // LIST]),
                 res_t[:, r0 : r0 + width],
-                mybir.AluOpType.add,
+                ALU.add,
             )
             nc.sync.dma_start(out[:, r0 : r0 + width], summed[:])
             r0 = r0 + width

@@ -23,7 +23,7 @@ GPSIMD_PART = (False, False, False, True)
 SCALAR_LAST = (768, 1024,)
 PIECE = 128
 SLOT = (2, 0, 1, 3)
-OUT_PIECES = (512, 512, 512, 256, 128, 128)
+STORES = ((0, 256), (256, 128), (256, 128), (256, 128), (256, 128), (128, 0), (128, 0))
 
 
 def tile_picked_unmerge_gelu_e_kernel(tc, xT, w1, res, offs, own, out):
@@ -111,13 +111,22 @@ def tile_picked_unmerge_gelu_e_kernel(tc, xT, w1, res, offs, own, out):
             nc.scalar.activation(y[:, e : e + PIECE], acc[:], ACT.Gelu_apprx_tanh, bias=zero_bias[:])
 
         r0 = 0
-        for i, width in enumerate(OUT_PIECES):
+        for i, (by_scalar, by_vector) in enumerate(STORES):
+            width = by_scalar + by_vector
             summed = keep.tile([P, width], F32, name="summed_%d" % i)
-            nc.vector.tensor_tensor(
-                summed[:],
-                y[:].indirect(own_t[:, r0 // LIST : (r0 + width) // LIST]),
-                res_t[:, r0 : r0 + width],
-                ALU.add,
-            )
+            if by_scalar:
+                fetched = keep.tile([P, by_scalar], F32, name="fetched_%d" % i)
+                nc.scalar.activation(
+                    fetched[:], y[:].indirect(own_t[:, r0 // LIST : (r0 + by_scalar) // LIST]), ACT.Copy
+                )
+                nc.vector.tensor_tensor(summed[:, 0:by_scalar], fetched[:], res_t[:, r0 : r0 + by_scalar], ALU.add)
+            if by_vector:
+                r1 = r0 + by_scalar
+                nc.vector.tensor_tensor(
+                    summed[:, by_scalar:width],
+                    y[:].indirect(own_t[:, r1 // LIST : (r1 + by_vector) // LIST]),
+                    res_t[:, r1 : r1 + by_vector],
+                    ALU.add,
+                )
             nc.sync.dma_start(out[:, r0 : r0 + width], summed[:])
             r0 = r0 + width

@@ -23,7 +23,7 @@ GPSIMD_PART = (False, False, False, True)
 SCALAR_LAST = (768, 1024,)
 PIECE = 128
 SLOT = (2, 0, 1, 3)
-STORES = ((0, 256), (256, 128), (256, 128), (256, 128), (256, 128), (128, 0), (128, 0))
+STORES = ((0, 384), (384, 0), (0, 192), (384, 0), (0, 192), (320, 0), (192, 0))
 
 
 def tile_picked_unmerge_gelu_e_kernel(tc, xT, w1, res, offs, own, out):

@@ -23,7 +23,7 @@ GPSIMD_PART = (False, False, False, True)
 SCALAR_LAST = (768, 1024,)
 PIECE = 128
 SLOT = (2, 0, 1, 3)
-STORES = ((0, 384), (384, 0), (0, 192), (384, 0), (0, 192), (320, 0), (192, 0))
+STORES = ((0, 448), (320, 0), (0, 224), (384, 0), (0, 160), (320, 0), (192, 0))
 
 
 def tile_picked_unmerge_gelu_e_kernel(tc, xT, w1, res, offs, own, out):

@@ -17,7 +17,7 @@ ALU = mybir.AluOpType
 P = 128
 PACK = 4
 LIST = 16
-VECTOR_PICKS = (352, 352, 352, 384)
+VECTOR_PICKS = (352, 352, 352, 416)
 PARTS = ((1280,768,),(1280,768,),(1408,640,),(576,704,512,256,),)
 GPSIMD_PART = (False, False, False, True)
 SCALAR_LAST = (768, 1024,)
@@ -49,8 +49,10 @@ def tile_picked_unmerge_gelu_e_kernel(tc, xT, w1, res, offs, own, out):
                 c0 = c0 + width
             if j == 0:
                 nc.sync.dma_start(offs_t[:], offs)
-        w_f32 = keep.tile([P, PACK, N], F32, name="w_f32", align_bytes=64)
-        nc.sync.dma_start(w_f32[:], w1.rearrange("(p j) n -> p j n", j=PACK))
+        w_rows = w1.rearrange("(p h j) n -> p h j n", h=2, j=2)
+        w_f32 = [keep.tile([P, 2, N], F32, name="w_f32_%d" % h) for h in range(2)]
+        for h in range(2):
+            nc.sync.dma_start(w_f32[h][:], w_rows[:, h])
         nc.sync.dma_start(own_t[:], own)
         res_t = keep.tile([P, U], F32, name="res_t")
         for h in range(2):
@@ -82,7 +84,10 @@ def tile_picked_unmerge_gelu_e_kernel(tc, xT, w1, res, offs, own, out):
         w_bf16 = keep.tile([P, N, PACK], BF16, name="w_bf16", tag="w_bf16_then_codes", align_bytes=64)
         w_codes = keep.tile([P, N], U32, name="w_codes", align_bytes=64)
         w_scales = keep.tile([P, N], U8, name="w_scales", align_bytes=64)
-        nc.gpsimd.tensor_scalar(w_bf16[:], w_f32[:].rearrange("p j n -> p n j"), 1.0, 0.0, ALU.mult, ALU.add)
+        for h in range(2):
+            nc.gpsimd.tensor_scalar(
+                w_bf16[:, :, 2 * h : 2 * h + 2], w_f32[h][:].rearrange("p j n -> p n j"), 1.0, 0.0, ALU.mult, ALU.add
+            )
         nc.vector.quantize_mx(
             out=w_codes[:].bitcast(FP8X4),
             scales=w_scales[:],

@@ -17,12 +17,12 @@ ALU = mybir.AluOpType
 P = 128
 PACK = 4
 LIST = 16
-VECTOR_PICKS = (352, 352, 352, 416)
-PARTS = ((1280,768,),(1280,768,),(1408,640,),(576,704,512,256,),)
-GPSIMD_PART = (False, False, False, True)
-SCALAR_LAST = (768, 1024,)
-PIECE = 128
-SLOT = (2, 0, 1, 3)
+EARLY_PICKS = 608
+THIRD_PICKS = 544
+LAST_PICKS = 416
+LAST_PARTS = (704, 704, 384, 256)
+SCALAR_LAST = (768, 1024)
+PIECES = (128, 128, 128, 128, 128, 128, 128, 128)
 STORES = ((0, 448), (320, 0), (0, 224), (384, 0), (0, 160), (320, 0), (192, 0))
 
 
@@ -35,6 +35,13 @@ def tile_picked_unmerge_gelu_e_kernel(tc, xT, w1, res, offs, own, out):
         offs_t = keep.tile([P, S // LIST], U16, name="offs_t")
         own_t = keep.tile([P, U // LIST], U16, name="own_t")
 
+        def entries(e0, e1):
+            return offs_t[:, e0 // LIST : e1 // LIST]
+
+        def halves(e0, e1):
+            mid = e0 + (e1 - e0) // 64 * 32
+            return ((e0, mid), (mid, e1))
+
         zero = keep.tile([P, 1], F32, name="zero")
         zero_bias = keep.tile([P, 1], F32, name="zero_bias")
         nc.vector.memset(zero[:], 0.0)
@@ -42,13 +49,14 @@ def tile_picked_unmerge_gelu_e_kernel(tc, xT, w1, res, offs, own, out):
 
         x_rows = xT.rearrange("(p j) t -> p j t", j=PACK)
         x_f32 = [keep.tile([P, T], F32, name="x_f32_%d" % j) for j in range(PACK)]
-        for j in range(PACK):
-            c0 = 0
-            for width in PARTS[j]:
-                nc.sync.dma_start(x_f32[j][:, c0 : c0 + width], x_rows[:, SLOT[j], c0 : c0 + width])
-                c0 = c0 + width
+        for j in range(PACK - 1):
+            nc.sync.dma_start(x_f32[j][:], x_rows[:, j])
             if j == 0:
                 nc.sync.dma_start(offs_t[:], offs)
+        c0 = 0
+        for width in LAST_PARTS:
+            nc.sync.dma_start(x_f32[3][:, c0 : c0 + width], x_rows[:, 3, c0 : c0 + width])
+            c0 = c0 + width
         w_rows = w1.rearrange("(p h j) n -> p h j n", h=2, j=2)
         w_f32 = [keep.tile([P, 2, N], F32, name="w_f32_%d" % h) for h in range(2)]
         for h in range(2):
@@ -61,25 +69,36 @@ def tile_picked_unmerge_gelu_e_kernel(tc, xT, w1, res, offs, own, out):
         picked = keep.tile([P, S * PACK], BF16, name="picked", align_bytes=64)
         slots = picked[:].rearrange("p (n j) -> p n j", j=PACK)
 
-        for j in range(PACK):
-            x_bf16 = keep.tile([P, T], BF16, name="x_bf16_%d" % j, tag="x_bf16_%d" % (j % 3))
-            c0 = 0
-            for i, width in enumerate(PARTS[j]):
-                if i == 0 and GPSIMD_PART[j]:
-                    nc.gpsimd.tensor_scalar(x_bf16[:, 0:width], x_f32[j][:, 0:width], 1.0, 0.0, ALU.mult, ALU.add)
-                else:
-                    nc.vector.tensor_copy(x_bf16[:, c0 : c0 + width], x_f32[j][:, c0 : c0 + width])
-                c0 = c0 + width
-            share = VECTOR_PICKS[j]
-            nc.vector.tensor_copy(slots[:, 0:share, SLOT[j]], x_f32[j][:].indirect(offs_t[:, 0 : share // LIST]))
-            e0 = share
-            for e1 in SCALAR_LAST if j == PACK - 1 else (S,):
-                nc.scalar.activation(
-                    slots[:, e0:e1, SLOT[j]],
-                    x_bf16[:].indirect(offs_t[:, e0 // LIST : e1 // LIST]),
-                    ACT.Copy,
+        flat_01 = keep.tile([P, 2, S], BF16, name="flat_01")
+        for j in range(2):
+            nc.vector.tensor_copy(slots[:, 0:EARLY_PICKS, j], x_f32[j][:].indirect(entries(0, EARLY_PICKS)))
+            for e0, e1 in halves(EARLY_PICKS, S):
+                nc.scalar.activation(flat_01[:, j, e0:e1], x_f32[j][:].indirect(entries(e0, e1)), ACT.Copy)
+        for e0, e1 in halves(EARLY_PICKS, S):
+            nc.scalar.activation(slots[:, e0:e1, 0:2], flat_01[:, :, e0:e1].rearrange("p j n -> p n j"), ACT.Copy)
+
+        flat_2 = keep.tile([P, S], BF16, name="flat_2")
+        nc.vector.tensor_copy(slots[:, 0:THIRD_PICKS, 2], x_f32[2][:].indirect(entries(0, THIRD_PICKS)))
+        for e0, e1 in halves(THIRD_PICKS, S):
+            nc.scalar.activation(flat_2[:, e0:e1], x_f32[2][:].indirect(entries(e0, e1)), ACT.Copy)
+        for e0, e1 in halves(THIRD_PICKS, S):
+            nc.scalar.activation(slots[:, e0:e1, 2], flat_2[:, e0:e1], ACT.Copy)
+
+        x_bf16 = keep.tile([P, T], BF16, name="x_bf16")
+        c0 = 0
+        for i, width in enumerate(LAST_PARTS):
+            if i < 1:
+                nc.gpsimd.tensor_scalar(
+                    x_bf16[:, c0 : c0 + width], x_f32[3][:, c0 : c0 + width], 1.0, 0.0, ALU.mult, ALU.add
                 )
-                e0 = e1
+            else:
+                nc.vector.tensor_copy(x_bf16[:, c0 : c0 + width], x_f32[3][:, c0 : c0 + width])
+            c0 = c0 + width
+        nc.vector.tensor_copy(slots[:, 0:LAST_PICKS, 3], x_f32[3][:].indirect(entries(0, LAST_PICKS)))
+        e0 = LAST_PICKS
+        for e1 in SCALAR_LAST:
+            nc.scalar.activation(slots[:, e0:e1, 3], x_bf16[:].indirect(entries(e0, e1)), ACT.Copy)
+            e0 = e1
 
         w_bf16 = keep.tile([P, N, PACK], BF16, name="w_bf16", tag="w_bf16_then_codes", align_bytes=64)
         w_codes = keep.tile([P, N], U32, name="w_codes", align_bytes=64)
@@ -96,16 +115,17 @@ def tile_picked_unmerge_gelu_e_kernel(tc, xT, w1, res, offs, own, out):
         all_codes = keep.tile([P, S], U32, name="all_codes", tag="w_bf16_then_codes", align_bytes=64)
 
         y = keep.tile([P, S], F32, name="y")
-        for g in range(S // PIECE):
-            e = g * PIECE
-            acc = psum.tile([P, PIECE], F32, name="acc_%d" % g)
-            codes = all_codes[:, e : e + PIECE]
-            scales = keep.tile([P, PIECE], U8, name="scales_%d" % g, align_bytes=64)
+        banks = [psum.tile([P, 128], F32, name="acc_%d" % g) for g in range(8)]
+        e = 0
+        for g, piece in enumerate(PIECES):
+            acc = banks[g % 8][:, 0:piece]
+            codes = all_codes[:, e : e + piece]
+            scales = keep.tile([P, piece], U8, name="scales_%d" % g, align_bytes=64)
             nc.vector.quantize_mx(
-                out=codes.bitcast(FP8X4), scales=scales[:], in_=picked[:, e * PACK : (e + PIECE) * PACK]
+                out=codes.bitcast(FP8X4), scales=scales[:], in_=picked[:, e * PACK : (e + piece) * PACK]
             )
             nc.tensor.matmul_mx(
-                out=acc[:],
+                out=acc,
                 lhsT=w_codes[:].bitcast(FP8X4),
                 lhsT_scale=w_scales[:],
                 rhs=codes.bitcast(FP8X4),
@@ -113,7 +133,8 @@ def tile_picked_unmerge_gelu_e_kernel(tc, xT, w1, res, offs, own, out):
                 start=True,
                 stop=True,
             )
-            nc.scalar.activation(y[:, e : e + PIECE], acc[:], ACT.Gelu_apprx_tanh, bias=zero_bias[:])
+            nc.scalar.activation(y[:, e : e + piece], acc, ACT.Gelu_apprx_tanh, bias=zero_bias[:])
+            e = e + piece
 
         r0 = 0
         for i, (by_scalar, by_vector) in enumerate(STORES):

@@ -17,10 +17,9 @@ ALU = mybir.AluOpType
 P = 128
 PACK = 4
 LIST = 16
-EARLY_PICKS = 608
-THIRD_PICKS = 544
+EARLY_PICKS = 576
 LAST_PICKS = 416
-LAST_PARTS = (704, 704, 384, 256)
+LAST_PARTS = (512, 448, 768, 320)
 SCALAR_LAST = (768, 1024)
 PIECES = (128, 128, 128, 128, 128, 128, 128, 128)
 STORES = ((0, 448), (320, 0), (0, 224), (384, 0), (0, 160), (320, 0), (192, 0))
@@ -69,25 +68,22 @@ def tile_picked_unmerge_gelu_e_kernel(tc, xT, w1, res, offs, own, out):
         picked = keep.tile([P, S * PACK], BF16, name="picked", align_bytes=64)
         slots = picked[:].rearrange("p (n j) -> p n j", j=PACK)
 
-        flat_01 = keep.tile([P, 2, S], BF16, name="flat_01")
-        for j in range(2):
+        flat = keep.tile([P, PACK - 1, S], BF16, name="flat")
+        for j in range(PACK - 1):
             nc.vector.tensor_copy(slots[:, 0:EARLY_PICKS, j], x_f32[j][:].indirect(entries(0, EARLY_PICKS)))
-            for e0, e1 in halves(EARLY_PICKS, S):
-                nc.scalar.activation(flat_01[:, j, e0:e1], x_f32[j][:].indirect(entries(e0, e1)), ACT.Copy)
+            for e0, e1 in halves(EARLY_PICKS, S) if j == PACK - 2 else ((EARLY_PICKS, S),):
+                nc.scalar.activation(flat[:, j, e0:e1], x_f32[j][:].indirect(entries(e0, e1)), ACT.Copy)
         for e0, e1 in halves(EARLY_PICKS, S):
-            nc.scalar.activation(slots[:, e0:e1, 0:2], flat_01[:, :, e0:e1].rearrange("p j n -> p n j"), ACT.Copy)
-
-        flat_2 = keep.tile([P, S], BF16, name="flat_2")
-        nc.vector.tensor_copy(slots[:, 0:THIRD_PICKS, 2], x_f32[2][:].indirect(entries(0, THIRD_PICKS)))
-        for e0, e1 in halves(THIRD_PICKS, S):
-            nc.scalar.activation(flat_2[:, e0:e1], x_f32[2][:].indirect(entries(e0, e1)), ACT.Copy)
-        for e0, e1 in halves(THIRD_PICKS, S):
-            nc.scalar.activation(slots[:, e0:e1, 2], flat_2[:, e0:e1], ACT.Copy)
+            nc.scalar.activation(
+                slots[:, e0:e1, 0 : PACK - 1].rearrange("p (c i) j -> p c j i", i=4),
+                flat[:, :, e0:e1].rearrange("p j (c i) -> p c j i", i=4),
+                ACT.Copy,
+            )
 
         x_bf16 = keep.tile([P, T], BF16, name="x_bf16")
         c0 = 0
         for i, width in enumerate(LAST_PARTS):
-            if i < 1:
+            if i < 2:
                 nc.gpsimd.tensor_scalar(
                     x_bf16[:, c0 : c0 + width], x_f32[3][:, c0 : c0 + width], 1.0, 0.0, ALU.mult, ALU.add
                 )

@@ -20,6 +20,7 @@ LIST = 16
 EARLY_PICKS = 576
 LAST_PICKS = 416
 LAST_PARTS = (512, 448, 768, 320)
+RES_PARTS = (448, 320, 224, 384, 480, 192,)
 SCALAR_LAST = (768, 1024)
 PIECES = (128, 128, 128, 128, 128, 128, 128, 128)
 STORES = ((0, 448), (320, 0), (0, 224), (384, 0), (0, 160), (320, 0), (192, 0))
@@ -62,8 +63,10 @@ def tile_picked_unmerge_gelu_e_kernel(tc, xT, w1, res, offs, own, out):
             nc.sync.dma_start(w_f32[h][:], w_rows[:, h])
         nc.sync.dma_start(own_t[:], own)
         res_t = keep.tile([P, U], F32, name="res_t")
-        for h in range(2):
-            nc.sync.dma_start(res_t[:, h * 1024 : (h + 1) * 1024], res[:, h * 1024 : (h + 1) * 1024])
+        c0 = 0
+        for width in RES_PARTS:
+            nc.sync.dma_start(res_t[:, c0 : c0 + width], res[:, c0 : c0 + width])
+            c0 = c0 + width
 
         picked = keep.tile([P, S * PACK], BF16, name="picked", align_bytes=64)
         slots = picked[:].rearrange("p (n j) -> p n j", j=PACK)

@@ -19,8 +19,8 @@ PACK = 4
 LIST = 16
 EARLY_PICKS = 576
 LAST_PICKS = 416
-LAST_PARTS = (512, 448, 768, 320)
-RES_PARTS = (448, 320, 224, 384, 480, 192,)
+LAST_PARTS = (704, 960, 384)
+RES_PARTS = (256, 256, 256, 256, 256, 256, 256, 256,)
 SCALAR_LAST = (768, 1024)
 PIECES = (128, 128, 128, 128, 128, 128, 128, 128)
 STORES = ((0, 448), (320, 0), (0, 224), (384, 0), (0, 160), (320, 0), (192, 0))
@@ -57,10 +57,8 @@ def tile_picked_unmerge_gelu_e_kernel(tc, xT, w1, res, offs, own, out):
         for width in LAST_PARTS:
             nc.sync.dma_start(x_f32[3][:, c0 : c0 + width], x_rows[:, 3, c0 : c0 + width])
             c0 = c0 + width
-        w_rows = w1.rearrange("(p h j) n -> p h j n", h=2, j=2)
-        w_f32 = [keep.tile([P, 2, N], F32, name="w_f32_%d" % h) for h in range(2)]
-        for h in range(2):
-            nc.sync.dma_start(w_f32[h][:], w_rows[:, h])
+        w_f32 = keep.tile([P, PACK, N], F32, name="w_f32")
+        nc.sync.dma_start(w_f32[:], w1.rearrange("(p j) n -> p j n", j=PACK))
         nc.sync.dma_start(own_t[:], own)
         res_t = keep.tile([P, U], F32, name="res_t")
         c0 = 0
@@ -86,7 +84,7 @@ def tile_picked_unmerge_gelu_e_kernel(tc, xT, w1, res, offs, own, out):
         x_bf16 = keep.tile([P, T], BF16, name="x_bf16")
         c0 = 0
         for i, width in enumerate(LAST_PARTS):
-            if i < 2:
+            if i < 1:
                 nc.gpsimd.tensor_scalar(
                     x_bf16[:, c0 : c0 + width], x_f32[3][:, c0 : c0 + width], 1.0, 0.0, ALU.mult, ALU.add
                 )
@@ -102,10 +100,7 @@ def tile_picked_unmerge_gelu_e_kernel(tc, xT, w1, res, offs, own, out):
         w_bf16 = keep.tile([P, N, PACK], BF16, name="w_bf16", tag="w_bf16_then_codes", align_bytes=64)
         w_codes = keep.tile([P, N], U32, name="w_codes", align_bytes=64)
         w_scales = keep.tile([P, N], U8, name="w_scales", align_bytes=64)
-        for h in range(2):
-            nc.gpsimd.tensor_scalar(
-                w_bf16[:, :, 2 * h : 2 * h + 2], w_f32[h][:].rearrange("p j n -> p n j"), 1.0, 0.0, ALU.mult, ALU.add
-            )
+        nc.gpsimd.tensor_scalar(w_bf16[:], w_f32[:].rearrange("p j n -> p n j"), 1.0, 0.0, ALU.mult, ALU.add)
         nc.vector.quantize_mx(
             out=w_codes[:].bitcast(FP8X4),
             scales=w_scales[:],

@@ -17,12 +17,12 @@ ALU = mybir.AluOpType
 P = 128
 PACK = 4
 LIST = 16
-EARLY_PICKS = 576
-LAST_PICKS = 416
-LAST_PARTS = (704, 960, 384)
-RES_PARTS = (256, 256, 256, 256, 256, 256, 256, 256,)
-SCALAR_LAST = (768, 1024)
-PIECES = (128, 128, 128, 128, 128, 128, 128, 128)
+EARLY_PICKS = 640
+LAST_PICKS = 544
+SLOT = (2, 0, 1, 3)
+LAST_GATHERS = (768, 1024,)
+LAST_INSERTS = (768, 896, 960, 1024,)
+PIECES = (128, 128, 128, 128, 128, 128, 128, 64, 64)
 STORES = ((0, 448), (320, 0), (0, 224), (384, 0), (0, 160), (320, 0), (192, 0))
 
 
@@ -48,32 +48,26 @@ def tile_picked_unmerge_gelu_e_kernel(tc, xT, w1, res, offs, own, out):
         nc.scalar.activation(zero_bias[:], zero[:], ACT.Gelu_apprx_tanh)
 
         x_rows = xT.rearrange("(p j) t -> p j t", j=PACK)
-        x_f32 = [keep.tile([P, T], F32, name="x_f32_%d" % j) for j in range(PACK)]
-        for j in range(PACK - 1):
-            nc.sync.dma_start(x_f32[j][:], x_rows[:, j])
+        x_f32 = [keep.tile([P, T], F32, name="x_f32_%d" % j, tag="x_f32_%d" % j) for j in range(PACK)]
+        for j in range(PACK):
+            nc.sync.dma_start(x_f32[j][:], x_rows[:, SLOT[j]])
             if j == 0:
                 nc.sync.dma_start(offs_t[:], offs)
-        c0 = 0
-        for width in LAST_PARTS:
-            nc.sync.dma_start(x_f32[3][:, c0 : c0 + width], x_rows[:, 3, c0 : c0 + width])
-            c0 = c0 + width
         w_f32 = keep.tile([P, PACK, N], F32, name="w_f32")
         nc.sync.dma_start(w_f32[:], w1.rearrange("(p j) n -> p j n", j=PACK))
         nc.sync.dma_start(own_t[:], own)
         res_t = keep.tile([P, U], F32, name="res_t")
-        c0 = 0
-        for width in RES_PARTS:
-            nc.sync.dma_start(res_t[:, c0 : c0 + width], res[:, c0 : c0 + width])
-            c0 = c0 + width
+        for h in range(2):
+            nc.sync.dma_start(res_t[:, h * 1024 : (h + 1) * 1024], res[:, h * 1024 : (h + 1) * 1024])
 
         picked = keep.tile([P, S * PACK], BF16, name="picked", align_bytes=64)
         slots = picked[:].rearrange("p (n j) -> p n j", j=PACK)
 
         flat = keep.tile([P, PACK - 1, S], BF16, name="flat")
         for j in range(PACK - 1):
-            nc.vector.tensor_copy(slots[:, 0:EARLY_PICKS, j], x_f32[j][:].indirect(entries(0, EARLY_PICKS)))
+            nc.vector.tensor_copy(slots[:, 0:EARLY_PICKS, SLOT[j]], x_f32[j][:].indirect(entries(0, EARLY_PICKS)))
             for e0, e1 in halves(EARLY_PICKS, S) if j == PACK - 2 else ((EARLY_PICKS, S),):
-                nc.scalar.activation(flat[:, j, e0:e1], x_f32[j][:].indirect(entries(e0, e1)), ACT.Copy)
+                nc.scalar.activation(flat[:, SLOT[j], e0:e1], x_f32[j][:].indirect(entries(e0, e1)), ACT.Copy)
         for e0, e1 in halves(EARLY_PICKS, S):
             nc.scalar.activation(
                 slots[:, e0:e1, 0 : PACK - 1].rearrange("p (c i) j -> p c j i", i=4),
@@ -81,20 +75,15 @@ def tile_picked_unmerge_gelu_e_kernel(tc, xT, w1, res, offs, own, out):
                 ACT.Copy,
             )
 
-        x_bf16 = keep.tile([P, T], BF16, name="x_bf16")
-        c0 = 0
-        for i, width in enumerate(LAST_PARTS):
-            if i < 1:
-                nc.gpsimd.tensor_scalar(
-                    x_bf16[:, c0 : c0 + width], x_f32[3][:, c0 : c0 + width], 1.0, 0.0, ALU.mult, ALU.add
-                )
-            else:
-                nc.vector.tensor_copy(x_bf16[:, c0 : c0 + width], x_f32[3][:, c0 : c0 + width])
-            c0 = c0 + width
+        flat_last = keep.tile([P, S], BF16, name="flat_last", tag="x_f32_0")
         nc.vector.tensor_copy(slots[:, 0:LAST_PICKS, 3], x_f32[3][:].indirect(entries(0, LAST_PICKS)))
         e0 = LAST_PICKS
-        for e1 in SCALAR_LAST:
-            nc.scalar.activation(slots[:, e0:e1, 3], x_bf16[:].indirect(entries(e0, e1)), ACT.Copy)
+        for e1 in LAST_GATHERS:
+            nc.scalar.activation(flat_last[:, e0:e1], x_f32[3][:].indirect(entries(e0, e1)), ACT.Copy)
+            e0 = e1
+        e0 = LAST_PICKS
+        for e1 in LAST_INSERTS:
+            nc.scalar.activation(slots[:, e0:e1, 3], flat_last[:, e0:e1], ACT.Copy)
             e0 = e1
 
         w_bf16 = keep.tile([P, N, PACK], BF16, name="w_bf16", tag="w_bf16_then_codes", align_bytes=64)

@@ -17,17 +17,33 @@ ALU = mybir.AluOpType
 P = 128
 PACK = 4
 LIST = 16
+BANKS = 8
+RUN = 4
+
+SLOT = (2, 0, 1, 3)
+
 EARLY_PICKS = 640
 LAST_PICKS = 544
-SLOT = (2, 0, 1, 3)
-LAST_GATHERS = (768, 1024,)
-LAST_INSERTS = (768, 896, 960, 1024,)
-PIECES = (128, 128, 128, 128, 128, 128, 128, 64, 64)
-STORES = ((0, 448), (320, 0), (0, 224), (384, 0), (0, 160), (320, 0), (192, 0))
+
+PIECES = (64,) + (128,) * 7 + (64,)
+LAST_GATHERS = (832, 1024)
+LAST_INSERTS = (704, 832, 960, 1024)
+
+STRETCHES = (
+    ("vector", 448),
+    ("scalar", 320),
+    ("vector", 224),
+    ("scalar", 384),
+    ("vector", 160),
+    ("scalar", 320),
+    ("scalar", 192),
+)
+RES_LOADS = 2
 
 
 def tile_picked_unmerge_gelu_e_kernel(tc, xT, w1, res, offs, own, out):
     nc = tc.nc
+    last = PACK - 1
     with ExitStack() as ctx:
         keep = ctx.enter_context(tc.tile_pool(name="keep", bufs=1))
         psum = ctx.enter_context(tc.psum_pool(name="psum", bufs=1))
@@ -38,53 +54,47 @@ def tile_picked_unmerge_gelu_e_kernel(tc, xT, w1, res, offs, own, out):
         def entries(e0, e1):
             return offs_t[:, e0 // LIST : e1 // LIST]
 
-        def halves(e0, e1):
-            mid = e0 + (e1 - e0) // 64 * 32
-            return ((e0, mid), (mid, e1))
-
         zero = keep.tile([P, 1], F32, name="zero")
         zero_bias = keep.tile([P, 1], F32, name="zero_bias")
         nc.vector.memset(zero[:], 0.0)
         nc.scalar.activation(zero_bias[:], zero[:], ACT.Gelu_apprx_tanh)
 
         x_rows = xT.rearrange("(p j) t -> p j t", j=PACK)
-        x_f32 = [keep.tile([P, T], F32, name="x_f32_%d" % j, tag="x_f32_%d" % j) for j in range(PACK)]
+        planes = [keep.tile([P, T], F32, name="plane_%d" % j, tag="plane_%d" % j) for j in range(PACK)]
         for j in range(PACK):
-            nc.sync.dma_start(x_f32[j][:], x_rows[:, SLOT[j]])
+            nc.sync.dma_start(planes[j][:], x_rows[:, SLOT[j]])
             if j == 0:
                 nc.sync.dma_start(offs_t[:], offs)
         w_f32 = keep.tile([P, PACK, N], F32, name="w_f32")
         nc.sync.dma_start(w_f32[:], w1.rearrange("(p j) n -> p j n", j=PACK))
         nc.sync.dma_start(own_t[:], own)
         res_t = keep.tile([P, U], F32, name="res_t")
-        for h in range(2):
-            nc.sync.dma_start(res_t[:, h * 1024 : (h + 1) * 1024], res[:, h * 1024 : (h + 1) * 1024])
+        for c0 in range(0, U, U // RES_LOADS):
+            nc.sync.dma_start(res_t[:, c0 : c0 + U // RES_LOADS], res[:, c0 : c0 + U // RES_LOADS])
 
         picked = keep.tile([P, S * PACK], BF16, name="picked", align_bytes=64)
         slots = picked[:].rearrange("p (n j) -> p n j", j=PACK)
 
-        flat = keep.tile([P, PACK - 1, S], BF16, name="flat")
-        for j in range(PACK - 1):
-            nc.vector.tensor_copy(slots[:, 0:EARLY_PICKS, SLOT[j]], x_f32[j][:].indirect(entries(0, EARLY_PICKS)))
-            for e0, e1 in halves(EARLY_PICKS, S) if j == PACK - 2 else ((EARLY_PICKS, S),):
-                nc.scalar.activation(flat[:, SLOT[j], e0:e1], x_f32[j][:].indirect(entries(e0, e1)), ACT.Copy)
-        for e0, e1 in halves(EARLY_PICKS, S):
+        middle = (EARLY_PICKS + S) // 2
+        halves = ((EARLY_PICKS, middle), (middle, S))
+        early_flat = keep.tile([P, last, S], BF16, name="early_flat")
+        for j in range(last):
+            nc.vector.tensor_copy(slots[:, 0:EARLY_PICKS, SLOT[j]], planes[j][:].indirect(entries(0, EARLY_PICKS)))
+            for e0, e1 in halves if j == last - 1 else ((EARLY_PICKS, S),):
+                nc.scalar.activation(early_flat[:, SLOT[j], e0:e1], planes[j][:].indirect(entries(e0, e1)), ACT.Copy)
+        for e0, e1 in halves:
             nc.scalar.activation(
-                slots[:, e0:e1, 0 : PACK - 1].rearrange("p (c i) j -> p c j i", i=4),
-                flat[:, :, e0:e1].rearrange("p j (c i) -> p c j i", i=4),
+                slots[:, e0:e1, 0:last].rearrange("p (c i) j -> p c j i", i=RUN),
+                early_flat[:, :, e0:e1].rearrange("p j (c i) -> p c j i", i=RUN),
                 ACT.Copy,
             )
 
-        flat_last = keep.tile([P, S], BF16, name="flat_last", tag="x_f32_0")
-        nc.vector.tensor_copy(slots[:, 0:LAST_PICKS, 3], x_f32[3][:].indirect(entries(0, LAST_PICKS)))
-        e0 = LAST_PICKS
-        for e1 in LAST_GATHERS:
-            nc.scalar.activation(flat_last[:, e0:e1], x_f32[3][:].indirect(entries(e0, e1)), ACT.Copy)
-            e0 = e1
-        e0 = LAST_PICKS
-        for e1 in LAST_INSERTS:
-            nc.scalar.activation(slots[:, e0:e1, 3], flat_last[:, e0:e1], ACT.Copy)
-            e0 = e1
+        last_flat = keep.tile([P, S], BF16, name="last_flat", tag="plane_0")
+        nc.vector.tensor_copy(slots[:, 0:LAST_PICKS, SLOT[last]], planes[last][:].indirect(entries(0, LAST_PICKS)))
+        for e0, e1 in zip((LAST_PICKS,) + LAST_GATHERS, LAST_GATHERS):
+            nc.scalar.activation(last_flat[:, e0:e1], planes[last][:].indirect(entries(e0, e1)), ACT.Copy)
+        for e0, e1 in zip((LAST_PICKS,) + LAST_INSERTS, LAST_INSERTS):
+            nc.scalar.activation(slots[:, e0:e1, SLOT[last]], last_flat[:, e0:e1], ACT.Copy)
 
         w_bf16 = keep.tile([P, N, PACK], BF16, name="w_bf16", tag="w_bf16_then_codes", align_bytes=64)
         w_codes = keep.tile([P, N], U32, name="w_codes", align_bytes=64)
@@ -95,47 +105,39 @@ def tile_picked_unmerge_gelu_e_kernel(tc, xT, w1, res, offs, own, out):
             scales=w_scales[:],
             in_=w_bf16[:].rearrange("p n j -> p (n j)"),
         )
-        all_codes = keep.tile([P, S], U32, name="all_codes", tag="w_bf16_then_codes", align_bytes=64)
 
+        x_codes = keep.tile([P, S], U32, name="x_codes", tag="w_bf16_then_codes", align_bytes=64)
         y = keep.tile([P, S], F32, name="y")
-        banks = [psum.tile([P, 128], F32, name="acc_%d" % g) for g in range(8)]
-        e = 0
+        banks = [psum.tile([P, max(PIECES)], F32, name="bank_%d" % b) for b in range(BANKS)]
+        e0 = 0
         for g, piece in enumerate(PIECES):
-            acc = banks[g % 8][:, 0:piece]
-            codes = all_codes[:, e : e + piece]
+            e1 = e0 + piece
+            acc = banks[g % BANKS][:, 0:piece]
+            codes = x_codes[:, e0:e1].bitcast(FP8X4)
             scales = keep.tile([P, piece], U8, name="scales_%d" % g, align_bytes=64)
-            nc.vector.quantize_mx(
-                out=codes.bitcast(FP8X4), scales=scales[:], in_=picked[:, e * PACK : (e + piece) * PACK]
-            )
+            nc.vector.quantize_mx(out=codes, scales=scales[:], in_=picked[:, e0 * PACK : e1 * PACK])
             nc.tensor.matmul_mx(
                 out=acc,
                 lhsT=w_codes[:].bitcast(FP8X4),
                 lhsT_scale=w_scales[:],
-                rhs=codes.bitcast(FP8X4),
+                rhs=codes,
                 rhs_scale=scales[:],
                 start=True,
                 stop=True,
             )
-            nc.scalar.activation(y[:, e : e + piece], acc, ACT.Gelu_apprx_tanh, bias=zero_bias[:])
-            e = e + piece
+            nc.scalar.activation(y[:, e0:e1], acc, ACT.Gelu_apprx_tanh, bias=zero_bias[:])
+            e0 = e1
 
         r0 = 0
-        for i, (by_scalar, by_vector) in enumerate(STORES):
-            width = by_scalar + by_vector
+        for i, (engine, width) in enumerate(STRETCHES):
+            r1 = r0 + width
+            looked_up = y[:].indirect(own_t[:, r0 // LIST : r1 // LIST])
             summed = keep.tile([P, width], F32, name="summed_%d" % i)
-            if by_scalar:
-                fetched = keep.tile([P, by_scalar], F32, name="fetched_%d" % i)
-                nc.scalar.activation(
-                    fetched[:], y[:].indirect(own_t[:, r0 // LIST : (r0 + by_scalar) // LIST]), ACT.Copy
-                )
-                nc.vector.tensor_tensor(summed[:, 0:by_scalar], fetched[:], res_t[:, r0 : r0 + by_scalar], ALU.add)
-            if by_vector:
-                r1 = r0 + by_scalar
-                nc.vector.tensor_tensor(
-                    summed[:, by_scalar:width],
-                    y[:].indirect(own_t[:, r1 // LIST : (r1 + by_vector) // LIST]),
-                    res_t[:, r1 : r1 + by_vector],
-                    ALU.add,
-                )
-            nc.sync.dma_start(out[:, r0 : r0 + width], summed[:])
-            r0 = r0 + width
+            if engine == "scalar":
+                fetched = keep.tile([P, width], F32, name="fetched_%d" % i)
+                nc.scalar.activation(fetched[:], looked_up, ACT.Copy)
+                nc.vector.tensor_tensor(summed[:], fetched[:], res_t[:, r0:r1], ALU.add)
+            else:
+                nc.vector.tensor_tensor(summed[:], looked_up, res_t[:, r0:r1], ALU.add)
+            nc.sync.dma_start(out[:, r0:r1], summed[:])
+            r0 = r1

@@ -18,16 +18,13 @@ P = 128
 PACK = 4
 LIST = 16
 BANKS = 8
-RUN = 4
 
 SLOT = (2, 0, 1, 3)
 
-EARLY_PICKS = 640
-LAST_PICKS = 544
+BORDER = (640, 512, 512, 640)
+LAST_GATHERS = (128, 384, 640)
 
-PIECES = (64,) + (128,) * 7 + (64,)
-LAST_GATHERS = (832, 1024)
-LAST_INSERTS = (704, 832, 960, 1024)
+PIECES = ((0, 128), (640, 128), (768, 128), (896, 128), (128, 128), (256, 128), (384, 128), (512, 64), (576, 64))
 
 STRETCHES = (
     ("vector", 448),
@@ -75,26 +72,11 @@ def tile_picked_unmerge_gelu_e_kernel(tc, xT, w1, res, offs, own, out):
         picked = keep.tile([P, S * PACK], BF16, name="picked", align_bytes=64)
         slots = picked[:].rearrange("p (n j) -> p n j", j=PACK)
 
-        middle = (EARLY_PICKS + S) // 2
-        halves = ((EARLY_PICKS, middle), (middle, S))
-        early_flat = keep.tile([P, last, S], BF16, name="early_flat")
-        for j in range(last):
-            nc.vector.tensor_copy(slots[:, 0:EARLY_PICKS, SLOT[j]], planes[j][:].indirect(entries(0, EARLY_PICKS)))
-            for e0, e1 in halves if j == last - 1 else ((EARLY_PICKS, S),):
-                nc.scalar.activation(early_flat[:, SLOT[j], e0:e1], planes[j][:].indirect(entries(e0, e1)), ACT.Copy)
-        for e0, e1 in halves:
-            nc.scalar.activation(
-                slots[:, e0:e1, 0:last].rearrange("p (c i) j -> p c j i", i=RUN),
-                early_flat[:, :, e0:e1].rearrange("p j (c i) -> p c j i", i=RUN),
-                ACT.Copy,
-            )
-
-        last_flat = keep.tile([P, S], BF16, name="last_flat", tag="plane_0")
-        nc.vector.tensor_copy(slots[:, 0:LAST_PICKS, SLOT[last]], planes[last][:].indirect(entries(0, LAST_PICKS)))
-        for e0, e1 in zip((LAST_PICKS,) + LAST_GATHERS, LAST_GATHERS):
-            nc.scalar.activation(last_flat[:, e0:e1], planes[last][:].indirect(entries(e0, e1)), ACT.Copy)
-        for e0, e1 in zip((LAST_PICKS,) + LAST_INSERTS, LAST_INSERTS):
-            nc.scalar.activation(slots[:, e0:e1, SLOT[last]], last_flat[:, e0:e1], ACT.Copy)
+        for j in range(PACK):
+            cuts = (0,) + (LAST_GATHERS if j == last else (BORDER[j],))
+            for e0, e1 in zip(cuts, cuts[1:]):
+                nc.scalar.activation(slots[:, e0:e1, SLOT[j]], planes[j][:].indirect(entries(e0, e1)), ACT.Copy)
+            nc.vector.tensor_copy(slots[:, BORDER[j] : S, SLOT[j]], planes[j][:].indirect(entries(BORDER[j], S)))
 
         w_bf16 = keep.tile([P, N, PACK], BF16, name="w_bf16", tag="w_bf16_then_codes", align_bytes=64)
         w_codes = keep.tile([P, N], U32, name="w_codes", align_bytes=64)
@@ -107,13 +89,13 @@ def tile_picked_unmerge_gelu_e_kernel(tc, xT, w1, res, offs, own, out):
         )
 
         x_codes = keep.tile([P, S], U32, name="x_codes", tag="w_bf16_then_codes", align_bytes=64)
+        first_codes = keep.tile([P, PIECES[0][1]], U32, name="first_codes", align_bytes=64)
         y = keep.tile([P, S], F32, name="y")
-        banks = [psum.tile([P, max(PIECES)], F32, name="bank_%d" % b) for b in range(BANKS)]
-        e0 = 0
-        for g, piece in enumerate(PIECES):
+        banks = [psum.tile([P, P], F32, name="bank_%d" % b) for b in range(BANKS)]
+        for g, (e0, piece) in enumerate(PIECES):
             e1 = e0 + piece
             acc = banks[g % BANKS][:, 0:piece]
-            codes = x_codes[:, e0:e1].bitcast(FP8X4)
+            codes = (x_codes[:, e0:e1] if g else first_codes[:]).bitcast(FP8X4)
             scales = keep.tile([P, piece], U8, name="scales_%d" % g, align_bytes=64)
             nc.vector.quantize_mx(out=codes, scales=scales[:], in_=picked[:, e0 * PACK : e1 * PACK])
             nc.tensor.matmul_mx(
@@ -126,7 +108,6 @@ def tile_picked_unmerge_gelu_e_kernel(tc, xT, w1, res, offs, own, out):
                 stop=True,
             )
             nc.scalar.activation(y[:, e0:e1], acc, ACT.Gelu_apprx_tanh, bias=zero_bias[:])
-            e0 = e1
 
         r0 = 0
         for i, (engine, width) in enumerate(STRETCHES):

@@ -17,6 +17,7 @@ ALU = mybir.AluOpType
 P = 128
 PACK = 4
 LIST = 16
+RUN = 4
 BANKS = 8
 
 SLOT = (2, 0, 1, 3)
@@ -81,7 +82,14 @@ def tile_picked_unmerge_gelu_e_kernel(tc, xT, w1, res, offs, own, out):
         w_bf16 = keep.tile([P, N, PACK], BF16, name="w_bf16", tag="w_bf16_then_codes", align_bytes=64)
         w_codes = keep.tile([P, N], U32, name="w_codes", align_bytes=64)
         w_scales = keep.tile([P, N], U8, name="w_scales", align_bytes=64)
-        nc.gpsimd.tensor_scalar(w_bf16[:], w_f32[:].rearrange("p j n -> p n j"), 1.0, 0.0, ALU.mult, ALU.add)
+        nc.gpsimd.tensor_scalar(
+            w_bf16[:].rearrange("p (c i) j -> p c j i", i=RUN),
+            w_f32[:].rearrange("p j (c i) -> p c j i", i=RUN),
+            1.0,
+            0.0,
+            ALU.mult,
+            ALU.add,
+        )
         nc.vector.quantize_mx(
             out=w_codes[:].bitcast(FP8X4),
             scales=w_scales[:],

@@ -18,6 +18,7 @@ P = 128
 PACK = 4
 LIST = 16
 RUN = 4
+DMA_ALIGN = 256
 BANKS = 8
 
 SLOT = (2, 0, 1, 3)
@@ -58,15 +59,15 @@ def tile_picked_unmerge_gelu_e_kernel(tc, xT, w1, res, offs, own, out):
         nc.scalar.activation(zero_bias[:], zero[:], ACT.Gelu_apprx_tanh)
 
         x_rows = xT.rearrange("(p j) t -> p j t", j=PACK)
-        planes = [keep.tile([P, T], F32, name="plane_%d" % j, tag="plane_%d" % j) for j in range(PACK)]
+        planes = [keep.tile([P, T], F32, name="plane_%d" % j, align_bytes=DMA_ALIGN) for j in range(PACK)]
         for j in range(PACK):
             nc.sync.dma_start(planes[j][:], x_rows[:, SLOT[j]])
             if j == 0:
                 nc.sync.dma_start(offs_t[:], offs)
-        w_f32 = keep.tile([P, PACK, N], F32, name="w_f32")
+        w_f32 = keep.tile([P, PACK, N], F32, name="w_f32", align_bytes=DMA_ALIGN)
         nc.sync.dma_start(w_f32[:], w1.rearrange("(p j) n -> p j n", j=PACK))
         nc.sync.dma_start(own_t[:], own)
-        res_t = keep.tile([P, U], F32, name="res_t")
+        res_t = keep.tile([P, U], F32, name="res_t", align_bytes=DMA_ALIGN)
         for c0 in range(0, U, U // RES_LOADS):
             nc.sync.dma_start(res_t[:, c0 : c0 + U // RES_LOADS], res[:, c0 : c0 + U // RES_LOADS])
 
@@ -121,7 +122,7 @@ def tile_picked_unmerge_gelu_e_kernel(tc, xT, w1, res, offs, own, out):
         for i, (engine, width) in enumerate(STRETCHES):
             r1 = r0 + width
             looked_up = y[:].indirect(own_t[:, r0 // LIST : r1 // LIST])
-            summed = keep.tile([P, width], F32, name="summed_%d" % i)
+            summed = keep.tile([P, width], F32, name="summed_%d" % i, align_bytes=DMA_ALIGN)
             if engine == "scalar":
                 fetched = keep.tile([P, width], F32, name="fetched_%d" % i)
                 nc.scalar.activation(fetched[:], looked_up, ACT.Copy)

@@ -24,20 +24,21 @@ BANKS = 8
 SLOT = (2, 0, 1, 3)
 
 BORDER = (640, 512, 512, 640)
-LAST_GATHERS = (128, 384, 640)
+LAST_GATHERS = (128, 512, 640)
 
 PIECES = ((0, 128), (640, 128), (768, 128), (896, 128), (128, 128), (256, 128), (384, 128), (512, 64), (576, 64))
 
 STRETCHES = (
-    ("vector", 448),
-    ("scalar", 320),
-    ("vector", 224),
+    ("vector", 384),
+    ("scalar", 256),
+    ("vector", 256),
     ("scalar", 384),
-    ("vector", 160),
-    ("scalar", 320),
+    ("vector", 192),
+    ("scalar", 256),
     ("scalar", 192),
+    ("scalar", 128),
 )
-RES_LOADS = 2
+RES_LOADS = 1
 
 
 def tile_picked_unmerge_gelu_e_kernel(tc, xT, w1, res, offs, own, out):

@@ -24,17 +24,17 @@ BANKS = 8
 SLOT = (2, 0, 1, 3)
 
 BORDER = (640, 512, 512, 640)
-LAST_GATHERS = (128, 512, 640)
+LAST_GATHERS = (192, 448, 640)
 
-PIECES = ((0, 128), (640, 128), (768, 128), (896, 128), (128, 128), (256, 128), (384, 128), (512, 64), (576, 64))
+PIECES = ((0, 128), (128, 64), (640, 128), (768, 128), (896, 128), (192, 128), (320, 128), (448, 128), (576, 64))
 
 STRETCHES = (
-    ("vector", 384),
-    ("scalar", 256),
-    ("vector", 256),
+    ("vector", 512),
     ("scalar", 384),
     ("vector", 192),
-    ("scalar", 256),
+    ("scalar", 320),
+    ("vector", 128),
+    ("scalar", 192),
     ("scalar", 192),
     ("scalar", 128),
 )

@@ -59,6 +59,18 @@ def tile_picked_unmerge_gelu_e_kernel(tc, xT, w1, res, offs, own, out):
         nc.vector.memset(zero[:], 0.0)
         nc.scalar.activation(zero_bias[:], zero[:], ACT.Gelu_apprx_tanh)
 
+        warm_f32 = keep.tile([P, PACK, RUN * 2], F32, name="warm_f32")
+        warm_bf16 = keep.tile([P, RUN * 2, PACK], BF16, name="warm_bf16")
+        nc.vector.memset(warm_f32[:], 0.0)
+        nc.gpsimd.tensor_scalar(
+            warm_bf16[:].rearrange("p (c i) j -> p c j i", i=RUN),
+            warm_f32[:].rearrange("p j (c i) -> p c j i", i=RUN),
+            1.0,
+            0.0,
+            ALU.mult,
+            ALU.add,
+        )
+
         x_rows = xT.rearrange("(p j) t -> p j t", j=PACK)
         planes = [keep.tile([P, T], F32, name="plane_%d" % j, align_bytes=DMA_ALIGN) for j in range(PACK)]
         for j in range(PACK):

@@ -129,7 +129,7 @@ def tile_picked_unmerge_gelu_e_kernel(tc, xT, w1, res, offs, own, out):
                 start=True,
                 stop=True,
             )
-            nc.scalar.activation(y[:, e0:e1], acc, ACT.Gelu_apprx_tanh, bias=zero_bias[:])
+            nc.scalar.activation(y[:, e0:e1], acc, ACT.Gelu_apprx_tanh, bias=0.0 if g else zero_bias[:])
 
         r0 = 0
         for i, (engine, width) in enumerate(STRETCHES):

from contextlib import ExitStack

import concourse.mybir as mybir

K, T, S, N, U = 512, 2048, 1024, 128, 2048
FLOPS = 2 * K * N * S

F32 = mybir.dt.float32
BF16 = mybir.dt.bfloat16
U32 = mybir.dt.uint32
U16 = mybir.dt.uint16
U8 = mybir.dt.uint8
FP8X4 = mybir.dt.float8_e4m3fn_x4
ACT = mybir.ActivationFunctionType
ALU = mybir.AluOpType

P = 128
PACK = 4
LIST = 16
RUN = 4
DMA_ALIGN = 256
BANKS = 8

SLOT = (2, 0, 1, 3)

BORDER = (640, 512, 512, 640)
LAST_GATHERS = (192, 448, 640)

PIECES = ((0, 128), (128, 64), (640, 128), (768, 128), (896, 128), (192, 128), (320, 128), (448, 128), (576, 64))

STRETCHES = (
    ("vector", 512),
    ("scalar", 384),
    ("vector", 192),
    ("scalar", 320),
    ("vector", 128),
    ("scalar", 192),
    ("scalar", 192),
    ("scalar", 128),
)
RES_LOADS = 1


def tile_picked_unmerge_gelu_e_kernel(tc, xT, w1, res, offs, own, out):
    nc = tc.nc
    last = PACK - 1
    with ExitStack() as ctx:
        keep = ctx.enter_context(tc.tile_pool(name="keep", bufs=1))
        psum = ctx.enter_context(tc.psum_pool(name="psum", bufs=1))

        offs_t = keep.tile([P, S // LIST], U16, name="offs_t")
        own_t = keep.tile([P, U // LIST], U16, name="own_t")

        def entries(e0, e1):
            return offs_t[:, e0 // LIST : e1 // LIST]

        zero = keep.tile([P, 1], F32, name="zero")
        zero_bias = keep.tile([P, 1], F32, name="zero_bias")
        nc.vector.memset(zero[:], 0.0)
        nc.scalar.activation(zero_bias[:], zero[:], ACT.Gelu_apprx_tanh)

        warm_f32 = keep.tile([P, PACK, RUN * 2], F32, name="warm_f32")
        warm_bf16 = keep.tile([P, RUN * 2, PACK], BF16, name="warm_bf16")
        nc.vector.memset(warm_f32[:], 0.0)
        nc.gpsimd.tensor_scalar(
            warm_bf16[:].rearrange("p (c i) j -> p c j i", i=RUN),
            warm_f32[:].rearrange("p j (c i) -> p c j i", i=RUN),
            1.0,
            0.0,
            ALU.mult,
            ALU.add,
        )

        x_rows = xT.rearrange("(p j) t -> p j t", j=PACK)
        planes = [keep.tile([P, T], F32, name="plane_%d" % j, align_bytes=DMA_ALIGN) for j in range(PACK)]
        for j in range(PACK):
            nc.sync.dma_start(planes[j][:], x_rows[:, SLOT[j]])
            if j == 0:
                nc.sync.dma_start(offs_t[:], offs)
        w_f32 = keep.tile([P, PACK, N], F32, name="w_f32", align_bytes=DMA_ALIGN)
        nc.sync.dma_start(w_f32[:], w1.rearrange("(p j) n -> p j n", j=PACK))
        nc.sync.dma_start(own_t[:], own)
        res_t = keep.tile([P, U], F32, name="res_t", align_bytes=DMA_ALIGN)
        for c0 in range(0, U, U // RES_LOADS):
            nc.sync.dma_start(res_t[:, c0 : c0 + U // RES_LOADS], res[:, c0 : c0 + U // RES_LOADS])

        picked = keep.tile([P, S * PACK], BF16, name="picked", align_bytes=64)
        slots = picked[:].rearrange("p (n j) -> p n j", j=PACK)

        for j in range(PACK):
            cuts = (0,) + (LAST_GATHERS if j == last else (BORDER[j],))
            for e0, e1 in zip(cuts, cuts[1:]):
                nc.scalar.activation(slots[:, e0:e1, SLOT[j]], planes[j][:].indirect(entries(e0, e1)), ACT.Copy)
            nc.vector.tensor_copy(slots[:, BORDER[j] : S, SLOT[j]], planes[j][:].indirect(entries(BORDER[j], S)))

        w_bf16 = keep.tile([P, N, PACK], BF16, name="w_bf16", tag="w_bf16_then_codes", align_bytes=64)
        w_codes = keep.tile([P, N], U32, name="w_codes", align_bytes=64)
        w_scales = keep.tile([P, N], U8, name="w_scales", align_bytes=64)
        nc.gpsimd.tensor_scalar(
            w_bf16[:].rearrange("p (c i) j -> p c j i", i=RUN),
            w_f32[:].rearrange("p j (c i) -> p c j i", i=RUN),
            1.0,
            0.0,
            ALU.mult,
            ALU.add,
        )
        nc.vector.quantize_mx(
            out=w_codes[:].bitcast(FP8X4),
            scales=w_scales[:],
            in_=w_bf16[:].rearrange("p n j -> p (n j)"),
        )

        x_codes = keep.tile([P, S], U32, name="x_codes", tag="w_bf16_then_codes", align_bytes=64)
        first_codes = keep.tile([P, PIECES[0][1]], U32, name="first_codes", align_bytes=64)
        y = keep.tile([P, S], F32, name="y")
        banks = [psum.tile([P, P], F32, name="bank_%d" % b) for b in range(BANKS)]
        for g, (e0, piece) in enumerate(PIECES):
            e1 = e0 + piece
            acc = banks[g % BANKS][:, 0:piece]
            codes = (x_codes[:, e0:e1] if g else first_codes[:]).bitcast(FP8X4)
            scales = keep.tile([P, piece], U8, name="scales_%d" % g, align_bytes=64)
            nc.vector.quantize_mx(out=codes, scales=scales[:], in_=picked[:, e0 * PACK : e1 * PACK])
            nc.tensor.matmul_mx(
                out=acc,
                lhsT=w_codes[:].bitcast(FP8X4),
                lhsT_scale=w_scales[:],
                rhs=codes,
                rhs_scale=scales[:],
                start=True,
                stop=True,
            )
            nc.scalar.activation(y[:, e0:e1], acc, ACT.Gelu_apprx_tanh, bias=0.0 if g else zero_bias[:])

        r0 = 0
        for i, (engine, width) in enumerate(STRETCHES):
            r1 = r0 + width
            looked_up = y[:].indirect(own_t[:, r0 // LIST : r1 // LIST])
            summed = keep.tile([P, width], F32, name="summed_%d" % i, align_bytes=DMA_ALIGN)
            if engine == "scalar":
                fetched = keep.tile([P, width], F32, name="fetched_%d" % i)
                nc.scalar.activation(fetched[:], looked_up, ACT.Copy)
                nc.vector.tensor_tensor(summed[:], fetched[:], res_t[:, r0:r1], ALU.add)
            else:
                nc.vector.tensor_tensor(summed[:], looked_up, res_t[:, r0:r1], ALU.add)
            nc.sync.dma_start(out[:, r0:r1], summed[:])
            r0 = r1
